import numpy as np
import ml_dtypes


def mxq(x, axis, fmt="e4m3"):
    dtype, down = {"e4m3": (ml_dtypes.float8_e4m3fn, 7), "e5m2": (ml_dtypes.float8_e5m2, 14)}[fmt]
    v = np.moveaxis(np.asarray(x, np.float32).astype(ml_dtypes.bfloat16).astype(np.float64), axis, -1)
    blocks = v.reshape(v.shape[:-1] + (-1, 32))
    amax = np.abs(blocks).max(-1, keepdims=True)
    byte = np.maximum(np.where(amax > 0, np.frexp(amax)[1] - 1 + 127, 0) - down, 1)
    scale = np.exp2(byte - 127.0)
    codes = (blocks / scale).astype(np.float32).astype(dtype).astype(np.float64)
    return np.moveaxis((codes * scale).reshape(v.shape), -1, axis)


WIDE = False


def mx_kscale(k):
    if not WIDE:
        return np.ones(k)
    levels = np.array([24, -24, 12, -12, 0])
    if k % 512:
        return np.exp2(np.random.permutation(np.resize(levels, k // 32))).repeat(32)
    a = np.empty((k // 512, 16))
    for p in range(k // 512):
        a[p, :8] = np.random.permutation(np.resize(levels, 8))
        for g in range(8):
            far = levels[np.abs(levels - a[p, g]) >= 10]
            a[p, g + 8] = far[np.random.randint(len(far))]
    return np.exp2(a.ravel()).repeat(32)


def f64(x):
    return np.asarray(x).astype(np.float64)


def striped(idx):
    return np.tile(idx.reshape(-1, 16).T, (8, 1)).astype(np.uint16)


def unstriped(offs):
    return offs[:16].T.reshape(-1).astype(np.int64)


def striped8(idx):
    return np.concatenate([v.reshape(-1, 16).T for v in idx]).astype(np.uint16)


def unstriped8(offs):
    return np.stack([offs[16 * g:16 * g + 16].T.reshape(-1) for g in range(8)]).astype(np.int64)


E2M1 = np.array([0.0, 0.5, 1.0, 1.5, 2.0, 3.0, 4.0, 6.0, -0.0, -0.5, -1.0, -1.5, -2.0, -3.0, -4.0, -6.0])


def pack_weight(w, fmt):
    k, n = w.shape
    w = f64(np.asarray(w, np.float32).astype(ml_dtypes.bfloat16)).reshape(k // 32, 32, n)
    amax = np.abs(w).max(1)
    if fmt == "e4m3":
        byte = np.frexp(amax)[1] - 1 + 127 - 7
    else:
        mant, ex = np.frexp(amax / 6.0)
        byte = np.where(mant > 0.5, ex, ex - 1) + 127
    byte = np.clip(np.where(amax > 0, byte, 1), 1, 254)
    scaled = (w * np.exp2(127.0 - byte)[:, None, :]).reshape(k, n).astype(np.float32)
    by_word = np.ascontiguousarray(scaled.reshape(k // 512, 128, 4, n).transpose(0, 1, 3, 2))
    if fmt == "e4m3":
        words = by_word.astype(ml_dtypes.float8_e4m3fn).view(np.uint8)
    else:
        c = by_word.astype(ml_dtypes.float4_e2m1fn).view(np.uint8) & 0xF
        words = (c[..., 0::2] | (c[..., 1::2] << 4)).reshape(k // 512, 128, 2 * n)
    return np.ascontiguousarray(words), np.ascontiguousarray(byte.astype(np.uint8).reshape(k // 512, 16, n))


def unpack_weight(words, scales, fmt):
    g, _, n = scales.shape
    words = np.ascontiguousarray(words).reshape(g, 128, n, -1)
    if fmt == "e4m3":
        vals = words.view(ml_dtypes.float8_e4m3fn).astype(np.float64)
    else:
        nib = np.empty((g, 128, n, 4), np.uint8)
        nib[..., 0::2] = words & 0xF
        nib[..., 1::2] = words >> 4
        vals = E2M1[nib]
    vals = vals * np.repeat(np.exp2(scales.astype(np.float64) - 127.0), 8, axis=1)[..., None]
    return vals.transpose(0, 1, 3, 2).reshape(g * 512, n)


def planes(y):
    n, m = y.shape
    v = y.astype(np.float32).astype(ml_dtypes.bfloat16).astype(np.float64).reshape(n // 32, 32, m)
    top = np.abs(v).max(1)
    byte = np.clip(np.where(top > 0, np.frexp(top)[1] - 1 + 127 - 7, 1), 1, 254)
    codes = (v * np.exp2(127.0 - byte)[:, None, :]).reshape(n, m).astype(np.float32).astype(ml_dtypes.float8_e4m3fn).view(np.uint8)
    words = codes.reshape(n // 512, 128, 4, m).transpose(0, 1, 3, 2)
    return np.ascontiguousarray(words), np.ascontiguousarray(byte.astype(np.uint8).reshape(n // 512, 16, m))


def sigm(f):
    return 1.0 / (1.0 + np.exp(-np.maximum(f, -700.0)))


K, L, R, N, T, J = 512, 512, 512, 512, 2048, 1024


def setup_inputs():
    n = np.random.standard_normal
    s = mx_kscale(K)[:, None]
    s2 = mx_kscale(L)[:, None]
    u = mx_kscale(R)[:, None]
    p_tab = pack_weight(n((L, T)) * s2, "e4m3")
    p_wa = pack_weight(n((K, R)) / np.sqrt(K) / s * u.T, "e4m3")
    p_wb = pack_weight(n((L, R)) / np.sqrt(L) / s2, "e4m3")
    return {
        "tab_words": p_tab[0],
        "tab_scales": p_tab[1],
        "xT": (n((K, T)) * s).astype(np.float32),
        "wgt2": np.repeat(np.random.uniform(0.5, 2.0, (8, J)), 16, axis=0).astype(np.float32),
        "wa_words": p_wa[0],
        "wa_scales": p_wa[1],
        "wb_words": p_wb[0],
        "wb_scales": p_wb[1],
        "wd": (n((R, N)) / np.sqrt(R) / u).astype(np.float32),
        "res": (n((N, J))).astype(np.float32),
        "offs": striped(np.random.permutation(T)[:J]),
        "offs2": striped8(np.stack([np.random.permutation(T)[:J] for _ in range(8)])),
    }


def reference(tab_words, tab_scales, xT, wgt2, wa_words, wa_scales, wb_words, wb_scales, wd, res, offs, offs2):
    idx = unstriped(offs)
    idx2 = unstriped8(offs2)
    tab_ = unpack_weight(tab_words, tab_scales, "e4m3")[:, idx]
    rows = np.arange(K)
    xg = f64(wgt2)[rows // 4 % 128] * f64(xT)[rows[:, None], idx2[rows % 512 // 64]]
    xT_ = mxq(xg, 0, "e4m3")
    wa_ = unpack_weight(wa_words, wa_scales, "e4m3")
    wb_ = unpack_weight(wb_words, wb_scales, "e4m3")
    ya = wa_.T @ xT_
    yb = wb_.T @ tab_
    h = ya * sigm(yb)
    h_ = mxq(h, 0, "e4m3")
    wd_ = mxq(f64(wd), 0, "e4m3")
    y = wd_.T @ h_
    out_0 = f64(res) + y
    return (out_0,) + planes(out_0)

@@ -1,0 +1,218 @@
+from contextlib import ExitStack
+
+import concourse.mybir as mybir
+
+K, L, R, N, T, J = 512, 512, 512, 512, 2048, 1024
+FLOPS = 2 * (K * R + L * R + R * N) * J
+
+F32 = mybir.dt.float32
+BF16 = mybir.dt.bfloat16
+I32 = mybir.dt.int32
+U32 = mybir.dt.uint32
+U16 = mybir.dt.uint16
+U8 = mybir.dt.uint8
+FP8X4 = mybir.dt.float8_e4m3fn_x4
+MULT = mybir.AluOpType.mult
+ADD = mybir.AluOpType.add
+SIGMOID = mybir.ActivationFunctionType.Sigmoid
+
+P = 128
+PACK = 4
+QUADS = 4
+UNIT = 128
+CHUNK = 256
+BANK = 512
+CHUNKS = J // CHUNK
+LIST_COLS = CHUNK // 16
+
+
+def tile_list_htabg_gate_resP_kernel(
+    tc, tab_words, tab_scales, xT, wgt2, wa_words, wa_scales, wb_words, wb_scales, wd, res, offs, offs2,
+    out_0, out_1, out_2,
+):
+    nc = tc.nc
+    with ExitStack() as ctx:
+        keep = ctx.enter_context(tc.tile_pool(name="keep", bufs=1))
+        psum = ctx.enter_context(tc.psum_pool(name="psum", bufs=4))
+
+        def sb(name, shape, dtype):
+            return keep.tile(shape, dtype, name=name, align_bytes=64)
+
+        def words(ap):
+            return ap[0].rearrange("p c i -> p (c i)").bitcast(I32)
+
+        def load_scales(queue, tile, first, scales):
+            for q in range(QUADS):
+                queue.dma_start(
+                    out=tile[32 * q + first : 32 * q + first + 4, :].bitcast(I32),
+                    in_=scales[0, 4 * q : 4 * q + 4, :].bitcast(I32),
+                )
+
+        tab_list = sb("tab_list", [P, J // 16], U16)
+        head_lists = sb("head_lists", [P, J // 16], U16)
+        tabw = sb("tabw", [P, T], I32)
+        tabs = sb("tabs", [P, T], U8)
+        ws_raw = sb("ws_raw", [P, R], U8)
+        wa_raw = sb("wa_raw", [P, R], I32)
+        wb_raw = sb("wb_raw", [P, R], I32)
+        wgt = sb("wgt", [P, J], F32)
+        x = [sb(f"x{t}", [P, T], F32) for t in range(PACK)]
+        wd_raw = sb("wd_raw", [P, PACK, N], F32)
+        res_sb = [sb(f"res{u}", [P, PACK, J // 2], F32) for u in range(2)]
+
+        nc.gpsimd.memset(tabs[:].bitcast(I32), 0)
+        nc.vector.memset(ws_raw[:].bitcast(I32), 0)
+
+        x_rows = xT.rearrange("(p i) t -> p i t", i=PACK)
+        nc.sync.dma_start(tab_list[:], offs)
+        nc.sync.dma_start(head_lists[:], offs2)
+        nc.sync.dma_start(out=wb_raw[:], in_=words(wb_words))
+        nc.sync.dma_start(out=wa_raw[:], in_=words(wa_words))
+        load_scales(nc.sync, tabs, 0, tab_scales)
+        nc.sync.dma_start(out=tabw[:], in_=words(tab_words))
+        load_scales(nc.sync, ws_raw, 0, wb_scales)
+        nc.sync.dma_start(out=wgt[:], in_=wgt2)
+        nc.sync.dma_start(out=x[0][:], in_=x_rows[:, 0, :])
+        load_scales(nc.sync, ws_raw, 4, wa_scales)
+        for t in range(1, PACK):
+            nc.sync.dma_start(out=x[t][:], in_=x_rows[:, t, :])
+        nc.sync.dma_start(out=wd_raw[:], in_=wd.rearrange("(p i) n -> p i n", i=PACK))
+        res_rows = res.rearrange("(p i) j -> p i j", i=PACK)
+        for u in range(2):
+            nc.sync.dma_start(out=res_sb[u][:], in_=res_rows[:, :, u * J // 2 : (u + 1) * J // 2])
+
+        v_codes = sb("v_codes", [P, J], U32)
+        v_scales = sb("v_scales", [P, J], U8)
+        nc.vector.tensor_copy(v_scales[:], tabs[:].indirect(tab_list[:]))
+        nc.vector.tensor_copy(v_codes[:], tabw[:].bitcast(U32).indirect(tab_list[:]))
+
+        wa_codes = sb("wa_codes", [P, R], I32)
+        wb_codes = sb("wb_codes", [P, R], I32)
+        w_scales = sb("w_scales", [P, R], U8)
+
+        def deal(dst, src, run):
+            nc.vector.tensor_copy(
+                out=dst[:].rearrange("p (t c i) -> p c t i", t=PACK, i=run),
+                in_=src[:].rearrange("p (c i t) -> p c t i", t=PACK, i=run),
+            )
+
+        deal(wb_codes, wb_raw, 4)
+        deal(w_scales, ws_raw, 16)
+        deal(wa_codes, wa_raw, 4)
+
+        def product(bank, w_codes, w_plane, codes, scales):
+            for t in range(PACK):
+                cols = slice(t * P, (t + 1) * P)
+                nc.tensor.matmul_mx(
+                    out=bank(t), lhsT=w_codes[:, cols].bitcast(FP8X4), lhsT_scale=w_plane[:, cols],
+                    rhs=codes.bitcast(FP8X4), rhs_scale=scales, start=True, stop=True,
+                )
+
+        gate = []
+        for u in range(J // UNIT):
+            cols = slice(u * UNIT, (u + 1) * UNIT)
+            yb = psum.tile([P, PACK, UNIT], F32, name="yb", tag="outer")
+            product(lambda t: yb[:, t, :], wb_codes, w_scales[0:P, :], v_codes[:, cols], v_scales[:, cols])
+            g = sb(f"gate{u}", [P, UNIT, PACK], F32)
+            nc.scalar.activation(g[:], yb[:].rearrange("p t j -> p j t"), SIGMOID)
+            gate.append(g)
+
+        picked = sb("picked", [P, PACK, J], F32)
+        for t in range(PACK - 1):
+            nc.vector.tensor_tensor(picked[:, t, :], x[t][:].indirect(head_lists[:]), wgt[:], MULT)
+        for c in range(CHUNKS):
+            cols = slice(c * CHUNK, (c + 1) * CHUNK)
+            nc.vector.tensor_tensor(
+                picked[:, PACK - 1, cols],
+                x[PACK - 1][:].indirect(head_lists[:, c * LIST_COLS : (c + 1) * LIST_COLS]),
+                wgt[:, cols], MULT,
+            )
+
+        def weave(name, planes):
+            width = planes.shape[2]
+            woven = sb(name, [P, width * PACK], BF16)
+            nc.scalar.copy(
+                out=woven[:].rearrange("p (c i t) -> p c t i", t=PACK, i=4),
+                in_=planes.rearrange("p t (c i) -> p c t i", i=4),
+            )
+            return woven
+
+        def quantize(name, woven):
+            width = woven.shape[1] // PACK
+            codes = sb(name + "_codes", [P, width], I32)
+            scales = sb(name + "_scales", [P, width], U8)
+            nc.vector.quantize_mx(out=codes[:].bitcast(FP8X4), scales=scales[:], in_=woven[:])
+            return codes, scales
+
+        ya, hq, woven_out = {}, {}, {}
+        out_rows = out_0.rearrange("(p i) j -> p i j", i=PACK)
+        out_words = words(out_1)
+        out_scales = sb("out_scales", [P, J], U8)
+
+        def picks(c):
+            woven = weave(f"xb{c}", picked[:, :, c * CHUNK : (c + 1) * CHUNK])
+            codes, scales = quantize(f"x{c}", woven)
+            for s in range(CHUNK // UNIT):
+                cols = slice(s * UNIT, (s + 1) * UNIT)
+                bank = psum.tile([P, PACK, UNIT], F32, name="ya", tag="inner")
+                product(lambda t: bank[:, t, :], wa_codes, w_scales[4:P, :], codes[:, cols], scales[:, cols])
+                ya[c, s] = bank
+
+        def join(c):
+            hb = sb(f"hb{c}", [P, CHUNK * PACK], BF16)
+            for s in range(CHUNK // UNIT):
+                nc.vector.tensor_tensor(
+                    hb[:, s * UNIT * PACK : (s + 1) * UNIT * PACK].rearrange("p (j t) -> p j t", t=PACK),
+                    ya[c, s][:].rearrange("p t j -> p j t"),
+                    gate[c * (CHUNK // UNIT) + s][:], MULT,
+                )
+            hq[c] = quantize(f"h{c}", hb)
+
+        def second(at, width):
+            c, first = divmod(at, CHUNK)
+            codes, scales = hq[c]
+            per_bank = BANK // width
+            banks = [psum.tile([P, per_bank, width], F32, name="y", tag="outer") for u in range(PACK // per_bank)]
+            product(
+                lambda t: banks[t // per_bank][:, t % per_bank, :], wd_codes, wd_scales[:],
+                codes[:, first : first + width], scales[:, first : first + width],
+            )
+            result = sb(f"result{at}", [P, PACK, width], F32)
+            half, col = divmod(at, J // 2)
+            for u, bank in enumerate(banks):
+                rows = slice(u * per_bank, (u + 1) * per_bank)
+                nc.vector.tensor_tensor(result[:, rows, :], bank[:], res_sb[half][:, rows, col : col + width], ADD)
+            nc.sync.dma_start(out=out_rows[:, :, at : at + width], in_=result[:])
+            woven_out[at] = weave(f"ob{at}", result[:])
+
+        def planes(at, width):
+            cols = slice(at, at + width)
+            codes = sb(f"out_codes{at}", [P, width], I32)
+            nc.vector.quantize_mx(out=codes[:].bitcast(FP8X4), scales=out_scales[:, cols], in_=woven_out[at][:])
+            nc.sync.dma_start(out=out_words[:, cols], in_=codes[:])
+
+        picks(0)
+        picks(1)
+        wdb = sb("wdb", [P, N * PACK], BF16)
+        nc.scalar.copy(
+            out=wdb[:].rearrange("p (t m i) -> p m t i", t=PACK, i=PACK),
+            in_=wd_raw[:].rearrange("p i (m t) -> p m t i", t=PACK),
+        )
+        join(0)
+        wd_codes, wd_scales = quantize("wd", wdb)
+        spans = [(c * CHUNK, CHUNK) for c in range(CHUNKS - 1)] + [(J - CHUNK, UNIT), (J - UNIT, UNIT)]
+        for c in range(len(spans) + 1):
+            if c + 2 < CHUNKS:
+                picks(c + 2)
+            if c + 1 < CHUNKS:
+                join(c + 1)
+            if c < len(spans):
+                second(*spans[c])
+            if c >= 1:
+                planes(*spans[c - 1])
+        for q in range(QUADS):
+            queue = nc.sync if q % 2 == 0 else nc.scalar
+            queue.dma_start(
+                out=out_2[0, 4 * q : 4 * q + 4, :].bitcast(I32),
+                in_=out_scales[32 * q : 32 * q + 4, :].bitcast(I32),
+            )

@@ -41,10 +41,10 @@ def tile_list_htabg_gate_resP_kernel(
         def words(ap):
             return ap[0].rearrange("p c i -> p (c i)").bitcast(I32)
 
-        def load_scales(queue, tile, first, scales):
+        def load_scales(tile, scales):
             for q in range(QUADS):
-                queue.dma_start(
-                    out=tile[32 * q + first : 32 * q + first + 4, :].bitcast(I32),
+                nc.sync.dma_start(
+                    out=tile[32 * q : 32 * q + 4, :].bitcast(I32),
                     in_=scales[0, 4 * q : 4 * q + 4, :].bitcast(I32),
                 )
 
@@ -52,7 +52,8 @@ def tile_list_htabg_gate_resP_kernel(
         head_lists = sb("head_lists", [P, J // 16], U16)
         tabw = sb("tabw", [P, T], I32)
         tabs = sb("tabs", [P, T], U8)
-        ws_raw = sb("ws_raw", [P, R], U8)
+        was_raw = sb("was_raw", [P, R], U8)
+        wbs_raw = sb("wbs_raw", [P, R], U8)
         wa_raw = sb("wa_raw", [P, R], I32)
         wb_raw = sb("wb_raw", [P, R], I32)
         wgt = sb("wgt", [P, J], F32)
@@ -61,21 +62,21 @@ def tile_list_htabg_gate_resP_kernel(
         res_sb = [sb(f"res{u}", [P, PACK, J // 2], F32) for u in range(2)]
 
         nc.gpsimd.memset(tabs[:].bitcast(I32), 0)
-        nc.vector.memset(ws_raw[:].bitcast(I32), 0)
+        nc.vector.memset(wbs_raw[:].bitcast(I32), 0)
+        nc.vector.memset(was_raw[:].bitcast(I32), 0)
 
         x_rows = xT.rearrange("(p i) t -> p i t", i=PACK)
         nc.sync.dma_start(tab_list[:], offs)
-        nc.sync.dma_start(head_lists[:], offs2)
         nc.sync.dma_start(out=wb_raw[:], in_=words(wb_words))
-        nc.sync.dma_start(out=wa_raw[:], in_=words(wa_words))
-        load_scales(nc.sync, tabs, 0, tab_scales)
+        nc.sync.dma_start(head_lists[:], offs2)
+        load_scales(tabs, tab_scales)
         nc.sync.dma_start(out=tabw[:], in_=words(tab_words))
-        load_scales(nc.sync, ws_raw, 0, wb_scales)
         nc.sync.dma_start(out=wgt[:], in_=wgt2)
-        nc.sync.dma_start(out=x[0][:], in_=x_rows[:, 0, :])
-        load_scales(nc.sync, ws_raw, 4, wa_scales)
-        for t in range(1, PACK):
+        load_scales(wbs_raw, wb_scales)
+        for t in range(PACK):
             nc.sync.dma_start(out=x[t][:], in_=x_rows[:, t, :])
+        nc.sync.dma_start(out=wa_raw[:], in_=words(wa_words))
+        load_scales(was_raw, wa_scales)
         nc.sync.dma_start(out=wd_raw[:], in_=wd.rearrange("(p i) n -> p i n", i=PACK))
         res_rows = res.rearrange("(p i) j -> p i j", i=PACK)
         for u in range(2):
@@ -88,7 +89,8 @@ def tile_list_htabg_gate_resP_kernel(
 
         wa_codes = sb("wa_codes", [P, R], I32)
         wb_codes = sb("wb_codes", [P, R], I32)
-        w_scales = sb("w_scales", [P, R], U8)
+        wa_plane = sb("wa_plane", [P, R], U8)
+        wb_plane = sb("wb_plane", [P, R], U8)
 
         def deal(dst, src, run):
             nc.vector.tensor_copy(
@@ -97,8 +99,7 @@ def tile_list_htabg_gate_resP_kernel(
             )
 
         deal(wb_codes, wb_raw, 4)
-        deal(w_scales, ws_raw, 16)
-        deal(wa_codes, wa_raw, 4)
+        deal(wb_plane, wbs_raw, 16)
 
         def product(bank, w_codes, w_plane, codes, scales):
             for t in range(PACK):
@@ -112,7 +113,7 @@ def tile_list_htabg_gate_resP_kernel(
         for u in range(J // UNIT):
             cols = slice(u * UNIT, (u + 1) * UNIT)
             yb = psum.tile([P, PACK, UNIT], F32, name="yb", tag="outer")
-            product(lambda t: yb[:, t, :], wb_codes, w_scales[0:P, :], v_codes[:, cols], v_scales[:, cols])
+            product(lambda t: yb[:, t, :], wb_codes, wb_plane, v_codes[:, cols], v_scales[:, cols])
             g = sb(f"gate{u}", [P, UNIT, PACK], F32)
             nc.scalar.activation(g[:], yb[:].rearrange("p t j -> p j t"), SIGMOID)
             gate.append(g)
@@ -127,6 +128,9 @@ def tile_list_htabg_gate_resP_kernel(
                 x[PACK - 1][:].indirect(head_lists[:, c * LIST_COLS : (c + 1) * LIST_COLS]),
                 wgt[:, cols], MULT,
             )
+
+        deal(wa_codes, wa_raw, 4)
+        deal(wa_plane, was_raw, 16)
 
         def weave(name, planes):
             width = planes.shape[2]
@@ -155,7 +159,7 @@ def tile_list_htabg_gate_resP_kernel(
             for s in range(CHUNK // UNIT):
                 cols = slice(s * UNIT, (s + 1) * UNIT)
                 bank = psum.tile([P, PACK, UNIT], F32, name="ya", tag="inner")
-                product(lambda t: bank[:, t, :], wa_codes, w_scales[4:P, :], codes[:, cols], scales[:, cols])
+                product(lambda t: bank[:, t, :], wa_codes, wa_plane, codes[:, cols], scales[:, cols])
                 ya[c, s] = bank
 
         def join(c):
@@ -174,7 +178,7 @@ def tile_list_htabg_gate_resP_kernel(
             per_bank = BANK // width
             banks = [psum.tile([P, per_bank, width], F32, name="y", tag="outer") for u in range(PACK // per_bank)]
             product(
-                lambda t: banks[t // per_bank][:, t % per_bank, :], wd_codes, wd_scales[:],
+                lambda t: banks[t // per_bank][:, t % per_bank, :], wd_codes, wd_scales,
                 codes[:, first : first + width], scales[:, first : first + width],
             )
             result = sb(f"result{at}", [P, PACK, width], F32)

@@ -1,6 +1,7 @@
 from contextlib import ExitStack
 
 import concourse.mybir as mybir
+from concourse.masks import make_identity
 
 K, L, R, N, T, J = 512, 512, 512, 512, 2048, 1024
 FLOPS = 2 * (K * R + L * R + R * N) * J
@@ -24,6 +25,9 @@ CHUNK = 256
 BANK = 512
 CHUNKS = J // CHUNK
 LIST_COLS = CHUNK // 16
+HEADS = 8
+RUN = 8
+BLOCKS = J // P
 
 
 def tile_list_htabg_gate_resP_kernel(
@@ -61,26 +65,55 @@ def tile_list_htabg_gate_resP_kernel(
         wd_raw = sb("wd_raw", [P, PACK, N], F32)
         res_sb = [sb(f"res{u}", [P, PACK, J // 2], F32) for u in range(2)]
 
+        wgt_rows = sb("wgt_rows", [P, P], F32)
+        identity = sb("identity", [P, P], F32)
         nc.gpsimd.memset(tabs[:].bitcast(I32), 0)
+        make_identity(nc, identity[:])
+        nc.vector.memset(wgt_rows[:], 0.0)
         nc.vector.memset(wbs_raw[:].bitcast(I32), 0)
         nc.vector.memset(was_raw[:].bitcast(I32), 0)
 
         x_rows = xT.rearrange("(p i) t -> p i t", i=PACK)
         nc.sync.dma_start(tab_list[:], offs)
         nc.sync.dma_start(out=wb_raw[:], in_=words(wb_words))
-        nc.sync.dma_start(head_lists[:], offs2)
+        nc.sync.dma_start(
+            out=wgt_rows[: HEADS * BLOCKS, :],
+            in_=wgt2.rearrange("(g r) (b c) -> g r b c", r=P // HEADS, c=P)[:, 0, :, :],
+        )
         load_scales(tabs, tab_scales)
         nc.sync.dma_start(out=tabw[:], in_=words(tab_words))
-        nc.sync.dma_start(out=wgt[:], in_=wgt2)
+        nc.sync.dma_start(head_lists[:], offs2)
         load_scales(wbs_raw, wb_scales)
         for t in range(PACK):
             nc.sync.dma_start(out=x[t][:], in_=x_rows[:, t, :])
         nc.sync.dma_start(out=wa_raw[:], in_=words(wa_words))
         load_scales(was_raw, wa_scales)
-        nc.sync.dma_start(out=wd_raw[:], in_=wd.rearrange("(p i) n -> p i n", i=PACK))
+        wd_rows = wd.rearrange("(b t i) n -> t b i n", t=PACK, i=RUN)
+        for t in range(PACK):
+            nc.sync.dma_start(out=wd_raw[:, t, :], in_=wd_rows[t])
         res_rows = res.rearrange("(p i) j -> p i j", i=PACK)
         for u in range(2):
             nc.sync.dma_start(out=res_sb[u][:], in_=res_rows[:, :, u * J // 2 : (u + 1) * J // 2])
+
+        turned = psum.tile([P, P], F32, name="turned", tag="inner")
+        nc.tensor.transpose(turned[:], wgt_rows[:], identity[:])
+        by_head = turned[:, : HEADS * BLOCKS].rearrange("c (g b) -> c b g", b=BLOCKS)
+        spread = sb("spread", [P, BLOCKS, HEADS, P // HEADS], F32)
+        for half in range(2):
+            blocks = slice(half * PACK, (half + 1) * PACK)
+            nc.scalar.copy(
+                out=spread[:, blocks, :, :],
+                in_=by_head[:, blocks, :].unsqueeze(3).to_broadcast([P, PACK, HEADS, P // HEADS]),
+            )
+        for half in range(2):
+            back = psum.tile([P, PACK, P], F32, name="back", tag="inner")
+            for i in range(PACK):
+                nc.tensor.transpose(
+                    back[:, i, :], spread[:, half * PACK + i, :, :].rearrange("c g r -> c (g r)"), identity[:]
+                )
+            nc.scalar.copy(
+                out=wgt[:, half * BANK : (half + 1) * BANK], in_=back[:].rearrange("p i c -> p (i c)")
+            )
 
         v_codes = sb("v_codes", [P, J], U32)
         v_scales = sb("v_scales", [P, J], U8)
@@ -94,12 +127,12 @@ def tile_list_htabg_gate_resP_kernel(
 
         def deal(dst, src, run):
             nc.vector.tensor_copy(
-                out=dst[:].rearrange("p (t c i) -> p c t i", t=PACK, i=run),
-                in_=src[:].rearrange("p (c i t) -> p c t i", t=PACK, i=run),
+                out=dst.rearrange("p (t b i) -> p t b i", t=PACK, i=run),
+                in_=src.rearrange("p (b t i) -> p t b i", t=PACK, i=run),
             )
 
-        deal(wb_codes, wb_raw, 4)
-        deal(wb_plane, wbs_raw, 16)
+        deal(wb_codes[:], wb_raw[:], RUN)
+        deal(wb_plane[:].bitcast(I32), wbs_raw[:].bitcast(I32), RUN // 4)
 
         def product(bank, w_codes, w_plane, codes, scales):
             for t in range(PACK):
@@ -129,8 +162,8 @@ def tile_list_htabg_gate_resP_kernel(
                 wgt[:, cols], MULT,
             )
 
-        deal(wa_codes, wa_raw, 4)
-        deal(wa_plane, was_raw, 16)
+        deal(wa_codes[:], wa_raw[:], RUN)
+        deal(wa_plane[:].bitcast(I32), was_raw[:].bitcast(I32), RUN // 4)
 
         def weave(name, planes):
             width = planes.shape[2]

@@ -19,7 +19,6 @@ SIGMOID = mybir.ActivationFunctionType.Sigmoid
 
 P = 128
 PACK = 4
-QUADS = 4
 UNIT = 128
 CHUNK = 256
 BANK = 512
@@ -46,11 +45,8 @@ def tile_list_htabg_gate_resP_kernel(
             return ap[0].rearrange("p c i -> p (c i)").bitcast(I32)
 
         def load_scales(tile, scales):
-            for q in range(QUADS):
-                nc.sync.dma_start(
-                    out=tile[32 * q : 32 * q + 4, :].bitcast(I32),
-                    in_=scales[0, 4 * q : 4 * q + 4, :].bitcast(I32),
-                )
+            for r in range(4):
+                nc.sync.dma_start(out=tile[r:P:32, :].bitcast(I32), in_=scales[0, r:16:4, :].bitcast(I32))
 
         tab_list = sb("tab_list", [P, J // 16], U16)
         head_lists = sb("head_lists", [P, J // 16], U16)
@@ -247,9 +243,6 @@ def tile_list_htabg_gate_resP_kernel(
                 second(*spans[c])
             if c >= 1:
                 planes(*spans[c - 1])
-        for q in range(QUADS):
-            queue = nc.sync if q % 2 == 0 else nc.scalar
-            queue.dma_start(
-                out=out_2[0, 4 * q : 4 * q + 4, :].bitcast(I32),
-                in_=out_scales[32 * q : 32 * q + 4, :].bitcast(I32),
-            )
+        for r in range(4):
+            queue = nc.sync if r % 2 == 0 else nc.scalar
+            queue.dma_start(out=out_2[0, r:16:4, :].bitcast(I32), in_=out_scales[r:P:32, :].bitcast(I32))

@@ -165,8 +165,8 @@ def tile_list_htabg_gate_resP_kernel(
             width = planes.shape[2]
             woven = sb(name, [P, width * PACK], BF16)
             nc.scalar.copy(
-                out=woven[:].rearrange("p (c i t) -> p c t i", t=PACK, i=4),
-                in_=planes.rearrange("p t (c i) -> p c t i", i=4),
+                out=woven[:].rearrange("p (c i t) -> p c t i", t=PACK, i=2),
+                in_=planes.rearrange("p t (c i) -> p c t i", i=2),
             )
             return woven
 

@@ -38,8 +38,8 @@ def tile_list_htabg_gate_resP_kernel(
         keep = ctx.enter_context(tc.tile_pool(name="keep", bufs=1))
         psum = ctx.enter_context(tc.psum_pool(name="psum", bufs=4))
 
-        def sb(name, shape, dtype):
-            return keep.tile(shape, dtype, name=name, align_bytes=64)
+        def sb(name, shape, dtype, tag=None):
+            return keep.tile(shape, dtype, name=name, tag=tag or name, align_bytes=64)
 
         def words(ap):
             return ap[0].rearrange("p c i -> p (c i)").bitcast(I32)
@@ -161,47 +161,49 @@ def tile_list_htabg_gate_resP_kernel(
         deal(wa_codes[:], wa_raw[:], RUN)
         deal(wa_plane[:].bitcast(I32), was_raw[:].bitcast(I32), RUN // 4)
 
-        def weave(name, planes):
-            width = planes.shape[2]
-            woven = sb(name, [P, width * PACK], BF16)
+        def weave(woven, planes):
             nc.scalar.copy(
-                out=woven[:].rearrange("p (c i t) -> p c t i", t=PACK, i=2),
+                out=woven.rearrange("p (c i t) -> p c t i", t=PACK, i=2),
                 in_=planes.rearrange("p t (c i) -> p c t i", i=2),
             )
-            return woven
 
-        def quantize(name, woven):
+        def quantize(name, woven, tag=None):
             width = woven.shape[1] // PACK
-            codes = sb(name + "_codes", [P, width], I32)
+            codes = sb(name + "_codes", [P, width], I32, tag)
             scales = sb(name + "_scales", [P, width], U8)
-            nc.vector.quantize_mx(out=codes[:].bitcast(FP8X4), scales=scales[:], in_=woven[:])
+            nc.vector.quantize_mx(out=codes[:].bitcast(FP8X4), scales=scales[:], in_=woven)
             return codes, scales
 
-        ya, hq, woven_out = {}, {}, {}
+        rounded, ya, hb, hq, results, woven_out = {}, {}, {}, {}, {}, {}
         out_rows = out_0.rearrange("(p i) j -> p i j", i=PACK)
         out_words = words(out_1)
         out_scales = sb("out_scales", [P, J], U8)
 
-        def picks(c):
-            woven = weave(f"xb{c}", picked[:, :, c * CHUNK : (c + 1) * CHUNK])
-            codes, scales = quantize(f"x{c}", woven)
+        def round_picks(c, woven):
+            rounded[c] = woven
+            weave(woven, picked[:, :, c * CHUNK : (c + 1) * CHUNK])
+
+        def first(c):
+            codes, scales = quantize(f"x{c}", rounded[c])
             for s in range(CHUNK // UNIT):
                 cols = slice(s * UNIT, (s + 1) * UNIT)
                 bank = psum.tile([P, PACK, UNIT], F32, name="ya", tag="inner")
                 product(lambda t: bank[:, t, :], wa_codes, wa_plane, codes[:, cols], scales[:, cols])
                 ya[c, s] = bank
 
-        def join(c):
-            hb = sb(f"hb{c}", [P, CHUNK * PACK], BF16)
+        def join(c, woven):
+            hb[c] = woven
             for s in range(CHUNK // UNIT):
                 nc.vector.tensor_tensor(
-                    hb[:, s * UNIT * PACK : (s + 1) * UNIT * PACK].rearrange("p (j t) -> p j t", t=PACK),
+                    woven[:, s * UNIT * PACK : (s + 1) * UNIT * PACK].rearrange("p (j t) -> p j t", t=PACK),
                     ya[c, s][:].rearrange("p t j -> p j t"),
                     gate[c * (CHUNK // UNIT) + s][:], MULT,
                 )
-            hq[c] = quantize(f"h{c}", hb)
 
-        def second(at, width):
+        def quantize_h(c, tag=None):
+            hq[c] = quantize(f"h{c}", hb[c], tag)
+
+        def second(at, width, aside=False):
             c, first = divmod(at, CHUNK)
             codes, scales = hq[c]
             per_bank = BANK // width
@@ -210,13 +212,23 @@ def tile_list_htabg_gate_resP_kernel(
                 lambda t: banks[t // per_bank][:, t % per_bank, :], wd_codes, wd_scales,
                 codes[:, first : first + width], scales[:, first : first + width],
             )
-            result = sb(f"result{at}", [P, PACK, width], F32)
+            result = sb(f"result{at}", [P, PACK, width], F32, "wd_raw" if aside else None)
             half, col = divmod(at, J // 2)
             for u, bank in enumerate(banks):
                 rows = slice(u * per_bank, (u + 1) * per_bank)
-                nc.vector.tensor_tensor(result[:, rows, :], bank[:], res_sb[half][:, rows, col : col + width], ADD)
+                residual = res_sb[half][:, rows, col : col + width]
+                if aside:
+                    sums = sb(f"sums{u}", [P, per_bank, width], F32)
+                    nc.scalar.copy(out=sums[:], in_=bank[:])
+                    nc.gpsimd.tensor_tensor(result[:, rows, :], sums[:], residual, ADD)
+                else:
+                    nc.vector.tensor_tensor(result[:, rows, :], bank[:], residual, ADD)
             nc.sync.dma_start(out=out_rows[:, :, at : at + width], in_=result[:])
-            woven_out[at] = weave(f"ob{at}", result[:])
+            results[at] = result
+
+        def round_result(at):
+            woven_out[at] = sb(f"ob{at}", [P, results[at].shape[2] * PACK], BF16)
+            weave(woven_out[at][:], results[at][:])
 
         def planes(at, width):
             cols = slice(at, at + width)
@@ -224,25 +236,43 @@ def tile_list_htabg_gate_resP_kernel(
             nc.vector.quantize_mx(out=codes[:].bitcast(FP8X4), scales=out_scales[:, cols], in_=woven_out[at][:])
             nc.sync.dma_start(out=out_words[:, cols], in_=codes[:])
 
-        picks(0)
-        picks(1)
+        wide = CHUNK * PACK
+        for c in range(CHUNKS - 1):
+            round_picks(c, sb(f"xb{c}", [P, wide], BF16)[:])
         wdb = sb("wdb", [P, N * PACK], BF16)
         nc.scalar.copy(
             out=wdb[:].rearrange("p (t m i) -> p m t i", t=PACK, i=PACK),
             in_=wd_raw[:].rearrange("p i (m t) -> p m t i", t=PACK),
         )
-        join(0)
-        wd_codes, wd_scales = quantize("wd", wdb)
-        spans = [(c * CHUNK, CHUNK) for c in range(CHUNKS - 1)] + [(J - CHUNK, UNIT), (J - UNIT, UNIT)]
-        for c in range(len(spans) + 1):
-            if c + 2 < CHUNKS:
-                picks(c + 2)
-            if c + 1 < CHUNKS:
-                join(c + 1)
-            if c < len(spans):
-                second(*spans[c])
-            if c >= 1:
-                planes(*spans[c - 1])
+        behind_wd = sb("behind_wd", [P, 2 * wide], BF16, "wd_raw")
+        round_picks(3, behind_wd[:, :wide])
+        first(0)
+        first(1)
+        join(0, sb("hb0", [P, wide], BF16)[:])
+        first(2)
+        join(1, sb("hb1", [P, wide], BF16)[:])
+        quantize_h(0)
+        wd_codes, wd_scales = quantize("wd", wdb[:])
+        quantize_h(1)
+        join(2, behind_wd[:, wide:])
+        first(3)
+        quantize_h(2)
+        second(0, CHUNK, aside=True)
+        second(CHUNK, CHUNK)
+        round_result(CHUNK)
+        round_result(0)
+        join(3, sb("hb3", [P, wide], BF16)[:])
+        planes(CHUNK, CHUNK)
+        quantize_h(3, "sums1")
+        second(2 * CHUNK, CHUNK)
+        round_result(2 * CHUNK)
+        planes(0, CHUNK)
+        for at in (3 * CHUNK, 3 * CHUNK + UNIT):
+            second(at, UNIT)
+            round_result(at)
+        planes(2 * CHUNK, CHUNK)
+        planes(3 * CHUNK, UNIT)
+        planes(3 * CHUNK + UNIT, UNIT)
         for r in range(4):
             queue = nc.sync if r % 2 == 0 else nc.scalar
             queue.dma_start(out=out_2[0, r:16:4, :].bitcast(I32), in_=out_scales[r:P:32, :].bitcast(I32))

@@ -239,11 +239,11 @@ def tile_list_htabg_gate_resP_kernel(
         wide = CHUNK * PACK
         for c in range(CHUNKS - 1):
             round_picks(c, sb(f"xb{c}", [P, wide], BF16)[:])
-        wdb = sb("wdb", [P, N * PACK], BF16)
-        nc.scalar.copy(
-            out=wdb[:].rearrange("p (t m i) -> p m t i", t=PACK, i=PACK),
-            in_=wd_raw[:].rearrange("p i (m t) -> p m t i", t=PACK),
-        )
+        wdb = sb("wdb", [P, N * PACK], BF16, "was_raw")
+        wd_out = wdb[:].rearrange("p (t m i) -> p m t i", t=PACK, i=PACK)
+        wd_in = wd_raw[:].rearrange("p i (m t) -> p m t i", t=PACK)
+        nc.gpsimd.tensor_scalar(wd_out[:, :, 2:, :], wd_in[:, :, 2:, :], 1.0, 0.0, MULT, ADD)
+        nc.scalar.copy(out=wd_out[:, :, :2, :], in_=wd_in[:, :, :2, :])
         behind_wd = sb("behind_wd", [P, 2 * wide], BF16, "wd_raw")
         round_picks(3, behind_wd[:, :wide])
         first(0)

@@ -63,13 +63,16 @@ def tile_list_htabg_gate_resP_kernel(
 
         wgt_rows = sb("wgt_rows", [P, P], F32)
         identity = sb("identity", [P, P], F32)
-        nc.gpsimd.memset(tabs[:].bitcast(I32), 0)
-        make_identity(nc, identity[:])
-        nc.vector.memset(wgt_rows[:], 0.0)
+        nc.vector.memset(tabs[:].bitcast(I32), 0)
+        nc.vector.memset(identity[:], 0.0)
+        make_identity(nc, identity[:], nomemset=True)
+        nc.vector.memset(wgt_rows[HEADS * BLOCKS :, :], 0.0)
         nc.vector.memset(wbs_raw[:].bitcast(I32), 0)
         nc.vector.memset(was_raw[:].bitcast(I32), 0)
 
         x_rows = xT.rearrange("(p i) t -> p i t", i=PACK)
+        wd_rows = wd.rearrange("(b t i) n -> t b i n", t=PACK, i=RUN)
+        res_rows = res.rearrange("(p i) j -> p i j", i=PACK)
         nc.sync.dma_start(tab_list[:], offs)
         nc.sync.dma_start(out=wb_raw[:], in_=words(wb_words))
         nc.sync.dma_start(
@@ -84,10 +87,8 @@ def tile_list_htabg_gate_resP_kernel(
             nc.sync.dma_start(out=x[t][:], in_=x_rows[:, t, :])
         nc.sync.dma_start(out=wa_raw[:], in_=words(wa_words))
         load_scales(was_raw, wa_scales)
-        wd_rows = wd.rearrange("(b t i) n -> t b i n", t=PACK, i=RUN)
         for t in range(PACK):
             nc.sync.dma_start(out=wd_raw[:, t, :], in_=wd_rows[t])
-        res_rows = res.rearrange("(p i) j -> p i j", i=PACK)
         for u in range(2):
             nc.sync.dma_start(out=res_sb[u][:], in_=res_rows[:, :, u * J // 2 : (u + 1) * J // 2])
 
@@ -167,112 +168,106 @@ def tile_list_htabg_gate_resP_kernel(
                 in_=planes.rearrange("p t (c i) -> p c t i", i=2),
             )
 
-        def quantize(name, woven, tag=None):
+        def quantize(name, woven):
             width = woven.shape[1] // PACK
-            codes = sb(name + "_codes", [P, width], I32, tag)
+            codes = sb(name + "_codes", [P, width], I32)
             scales = sb(name + "_scales", [P, width], U8)
             nc.vector.quantize_mx(out=codes[:].bitcast(FP8X4), scales=scales[:], in_=woven)
             return codes, scales
 
-        rounded, ya, hb, hq, results, woven_out = {}, {}, {}, {}, {}, {}
         out_rows = out_0.rearrange("(p i) j -> p i j", i=PACK)
         out_words = words(out_1)
+        out_codes = sb("out_codes", [P, J], I32)
         out_scales = sb("out_scales", [P, J], U8)
+        wide = CHUNK * PACK
+        halves = CHUNK // UNIT
+        xb = [sb(f"xb{c}", [P, wide], BF16) for c in range(CHUNKS)]
+        hb = [sb(f"hb{c}", [P, wide], BF16) for c in range(CHUNKS)]
+        ob = [sb(f"ob{c}", [P, wide], BF16) for c in range(CHUNKS)]
+        result = [sb(f"result{c}", [P, PACK, CHUNK], F32) for c in range(CHUNKS)]
+        ya, y, hq = {}, {}, {}
 
-        def round_picks(c, woven):
-            rounded[c] = woven
-            weave(woven, picked[:, :, c * CHUNK : (c + 1) * CHUNK])
+        def products(banks, c, name, tag, w_codes, w_plane, codes, scales):
+            for s in range(halves):
+                cols = slice(s * UNIT, (s + 1) * UNIT)
+                bank = psum.tile([P, PACK, UNIT], F32, name=name, tag=tag)
+                product(lambda t: bank[:, t, :], w_codes, w_plane, codes[:, cols], scales[:, cols])
+                banks[c, s] = bank
 
         def first(c):
-            codes, scales = quantize(f"x{c}", rounded[c])
-            for s in range(CHUNK // UNIT):
-                cols = slice(s * UNIT, (s + 1) * UNIT)
-                bank = psum.tile([P, PACK, UNIT], F32, name="ya", tag="inner")
-                product(lambda t: bank[:, t, :], wa_codes, wa_plane, codes[:, cols], scales[:, cols])
-                ya[c, s] = bank
+            products(ya, c, "ya", "inner", wa_codes, wa_plane, *quantize(f"x{c}", xb[c][:]))
 
-        def join(c, woven):
-            hb[c] = woven
-            for s in range(CHUNK // UNIT):
+        def join(c):
+            for s in range(halves):
                 nc.vector.tensor_tensor(
-                    woven[:, s * UNIT * PACK : (s + 1) * UNIT * PACK].rearrange("p (j t) -> p j t", t=PACK),
+                    hb[c][:, s * UNIT * PACK : (s + 1) * UNIT * PACK].rearrange("p (j t) -> p j t", t=PACK),
                     ya[c, s][:].rearrange("p t j -> p j t"),
-                    gate[c * (CHUNK // UNIT) + s][:], MULT,
+                    gate[c * halves + s][:], MULT,
                 )
 
-        def quantize_h(c, tag=None):
-            hq[c] = quantize(f"h{c}", hb[c], tag)
+        def quantize_h(c):
+            hq[c] = quantize(f"h{c}", hb[c][:])
 
-        def second(at, width, aside=False):
-            c, first = divmod(at, CHUNK)
-            codes, scales = hq[c]
-            per_bank = BANK // width
-            banks = [psum.tile([P, per_bank, width], F32, name="y", tag="outer") for u in range(PACK // per_bank)]
-            product(
-                lambda t: banks[t // per_bank][:, t % per_bank, :], wd_codes, wd_scales,
-                codes[:, first : first + width], scales[:, first : first + width],
-            )
-            result = sb(f"result{at}", [P, PACK, width], F32, "wd_raw" if aside else None)
-            half, col = divmod(at, J // 2)
-            for u, bank in enumerate(banks):
-                rows = slice(u * per_bank, (u + 1) * per_bank)
-                residual = res_sb[half][:, rows, col : col + width]
-                if aside:
-                    sums = sb(f"sums{u}", [P, per_bank, width], F32)
-                    nc.scalar.copy(out=sums[:], in_=bank[:])
-                    nc.gpsimd.tensor_tensor(result[:, rows, :], sums[:], residual, ADD)
-                else:
-                    nc.vector.tensor_tensor(result[:, rows, :], bank[:], residual, ADD)
-            nc.sync.dma_start(out=out_rows[:, :, at : at + width], in_=result[:])
-            results[at] = result
+        def second(c):
+            products(y, c, "y", "outer", wd_codes, wd_scales, *hq[c])
 
-        def round_result(at):
-            woven_out[at] = sb(f"ob{at}", [P, results[at].shape[2] * PACK], BF16)
-            weave(woven_out[at][:], results[at][:])
+        def add(c):
+            for s in range(halves):
+                cols = slice(s * UNIT, (s + 1) * UNIT)
+                half, col = divmod(c * CHUNK + s * UNIT, J // 2)
+                nc.vector.tensor_tensor(
+                    result[c][:, :, cols], y[c, s][:], res_sb[half][:, :, col : col + UNIT], ADD
+                )
+                weave(ob[c][:, s * UNIT * PACK : (s + 1) * UNIT * PACK], result[c][:, :, cols])
+            nc.sync.dma_start(out=out_rows[:, :, c * CHUNK : (c + 1) * CHUNK], in_=result[c][:])
 
         def planes(at, width):
+            c, col = divmod(at, CHUNK)
             cols = slice(at, at + width)
-            codes = sb(f"out_codes{at}", [P, width], I32)
-            nc.vector.quantize_mx(out=codes[:].bitcast(FP8X4), scales=out_scales[:, cols], in_=woven_out[at][:])
-            nc.sync.dma_start(out=out_words[:, cols], in_=codes[:])
+            nc.vector.quantize_mx(
+                out=out_codes[:, cols].bitcast(FP8X4), scales=out_scales[:, cols],
+                in_=ob[c][:, col * PACK : (col + width) * PACK],
+            )
 
-        wide = CHUNK * PACK
-        for c in range(CHUNKS - 1):
-            round_picks(c, sb(f"xb{c}", [P, wide], BF16)[:])
-        wdb = sb("wdb", [P, N * PACK], BF16, "was_raw")
-        wd_out = wdb[:].rearrange("p (t m i) -> p m t i", t=PACK, i=PACK)
-        wd_in = wd_raw[:].rearrange("p i (m t) -> p m t i", t=PACK)
-        nc.gpsimd.tensor_scalar(wd_out[:, :, 2:, :], wd_in[:, :, 2:, :], 1.0, 0.0, MULT, ADD)
-        nc.scalar.copy(out=wd_out[:, :, :2, :], in_=wd_in[:, :, :2, :])
-        behind_wd = sb("behind_wd", [P, 2 * wide], BF16, "wd_raw")
-        round_picks(3, behind_wd[:, :wide])
+        def store_codes(lo, hi):
+            nc.sync.dma_start(out=out_words[:, lo:hi], in_=out_codes[:, lo:hi])
+
+        for c in range(CHUNKS):
+            weave(xb[c][:], picked[:, :, c * CHUNK : (c + 1) * CHUNK])
+        wdb = sb("wdb", [P, N * PACK], BF16)
+        nc.scalar.copy(
+            out=wdb[:].rearrange("p (t m i) -> p m t i", t=PACK, i=PACK),
+            in_=wd_raw[:].rearrange("p i (m t) -> p m t i", t=PACK),
+        )
         first(0)
         first(1)
-        join(0, sb("hb0", [P, wide], BF16)[:])
+        join(0)
         first(2)
-        join(1, sb("hb1", [P, wide], BF16)[:])
+        join(1)
+        first(3)
         quantize_h(0)
+        join(2)
         wd_codes, wd_scales = quantize("wd", wdb[:])
         quantize_h(1)
-        join(2, behind_wd[:, wide:])
-        first(3)
+        second(0)
+        second(1)
+        join(3)
+        add(0)
         quantize_h(2)
-        second(0, CHUNK, aside=True)
-        second(CHUNK, CHUNK)
-        round_result(CHUNK)
-        round_result(0)
-        join(3, sb("hb3", [P, wide], BF16)[:])
-        planes(CHUNK, CHUNK)
-        quantize_h(3, "sums1")
-        second(2 * CHUNK, CHUNK)
-        round_result(2 * CHUNK)
+        second(2)
+        add(1)
+        quantize_h(3)
+        second(3)
         planes(0, CHUNK)
-        for at in (3 * CHUNK, 3 * CHUNK + UNIT):
-            second(at, UNIT)
-            round_result(at)
+        add(2)
+        planes(CHUNK, CHUNK)
+        store_codes(0, 2 * CHUNK)
+        add(3)
         planes(2 * CHUNK, CHUNK)
         planes(3 * CHUNK, UNIT)
-        planes(3 * CHUNK + UNIT, UNIT)
+        store_codes(2 * CHUNK, J - UNIT)
+        planes(J - UNIT, UNIT)
+        store_codes(J - UNIT, J)
         for r in range(4):
             queue = nc.sync if r % 2 == 0 else nc.scalar
             queue.dma_start(out=out_2[0, r:16:4, :].bitcast(I32), in_=out_scales[r:P:32, :].bitcast(I32))

@@ -258,16 +258,14 @@ def tile_list_htabg_gate_resP_kernel(
         add(1)
         quantize_h(3)
         second(3)
-        planes(0, CHUNK)
         add(2)
-        planes(CHUNK, CHUNK)
-        store_codes(0, 2 * CHUNK)
         add(3)
+        planes(0, CHUNK)
+        planes(CHUNK, CHUNK)
         planes(2 * CHUNK, CHUNK)
+        store_codes(0, 3 * CHUNK)
         planes(3 * CHUNK, UNIT)
-        store_codes(2 * CHUNK, J - UNIT)
         planes(J - UNIT, UNIT)
-        store_codes(J - UNIT, J)
+        store_codes(3 * CHUNK, J)
         for r in range(4):
-            queue = nc.sync if r % 2 == 0 else nc.scalar
-            queue.dma_start(out=out_2[0, r:16:4, :].bitcast(I32), in_=out_scales[r:P:32, :].bitcast(I32))
+            nc.scalar.dma_start(out=out_2[0, r:16:4, :].bitcast(I32), in_=out_scales[r:P:32, :].bitcast(I32))

@@ -27,6 +27,8 @@ LIST_COLS = CHUNK // 16
 HEADS = 8
 RUN = 8
 BLOCKS = J // P
+WB_ROW = 4
+WA_ROW = 8
 
 
 def tile_list_htabg_gate_resP_kernel(
@@ -44,9 +46,9 @@ def tile_list_htabg_gate_resP_kernel(
         def words(ap):
             return ap[0].rearrange("p c i -> p (c i)").bitcast(I32)
 
-        def load_scales(tile, scales):
+        def load_scales(tile, scales, first=0):
             for r in range(4):
-                nc.sync.dma_start(out=tile[r:P:32, :].bitcast(I32), in_=scales[0, r:16:4, :].bitcast(I32))
+                nc.sync.dma_start(out=tile[first + r : P : 32, :].bitcast(I32), in_=scales[0, r:16:4, :].bitcast(I32))
 
         tab_list = sb("tab_list", [P, J // 16], U16)
         head_lists = sb("head_lists", [P, J // 16], U16)
@@ -64,9 +66,9 @@ def tile_list_htabg_gate_resP_kernel(
         wgt_rows = sb("wgt_rows", [P, P], F32)
         identity = sb("identity", [P, P], F32)
         nc.vector.memset(tabs[:].bitcast(I32), 0)
+        nc.vector.memset(wgt_rows[:], 0.0)
         nc.vector.memset(identity[:], 0.0)
         make_identity(nc, identity[:], nomemset=True)
-        nc.vector.memset(wgt_rows[HEADS * BLOCKS :, :], 0.0)
         nc.vector.memset(wbs_raw[:].bitcast(I32), 0)
         nc.vector.memset(was_raw[:].bitcast(I32), 0)
 
@@ -75,18 +77,18 @@ def tile_list_htabg_gate_resP_kernel(
         res_rows = res.rearrange("(p i) j -> p i j", i=PACK)
         nc.sync.dma_start(tab_list[:], offs)
         nc.sync.dma_start(out=wb_raw[:], in_=words(wb_words))
+        load_scales(tabs, tab_scales)
         nc.sync.dma_start(
             out=wgt_rows[: HEADS * BLOCKS, :],
             in_=wgt2.rearrange("(g r) (b c) -> g r b c", r=P // HEADS, c=P)[:, 0, :, :],
         )
-        load_scales(tabs, tab_scales)
         nc.sync.dma_start(out=tabw[:], in_=words(tab_words))
         nc.sync.dma_start(head_lists[:], offs2)
-        load_scales(wbs_raw, wb_scales)
+        load_scales(wbs_raw, wb_scales, WB_ROW)
         for t in range(PACK):
             nc.sync.dma_start(out=x[t][:], in_=x_rows[:, t, :])
         nc.sync.dma_start(out=wa_raw[:], in_=words(wa_words))
-        load_scales(was_raw, wa_scales)
+        load_scales(was_raw, wa_scales, WA_ROW)
         for t in range(PACK):
             nc.sync.dma_start(out=wd_raw[:, t, :], in_=wd_rows[t])
         for u in range(2):
@@ -143,7 +145,7 @@ def tile_list_htabg_gate_resP_kernel(
         for u in range(J // UNIT):
             cols = slice(u * UNIT, (u + 1) * UNIT)
             yb = psum.tile([P, PACK, UNIT], F32, name="yb", tag="outer")
-            product(lambda t: yb[:, t, :], wb_codes, wb_plane, v_codes[:, cols], v_scales[:, cols])
+            product(lambda t: yb[:, t, :], wb_codes, wb_plane[WB_ROW:, :], v_codes[:, cols], v_scales[:, cols])
             g = sb(f"gate{u}", [P, UNIT, PACK], F32)
             nc.scalar.activation(g[:], yb[:].rearrange("p t j -> p j t"), SIGMOID)
             gate.append(g)
@@ -195,7 +197,7 @@ def tile_list_htabg_gate_resP_kernel(
                 banks[c, s] = bank
 
         def first(c):
-            products(ya, c, "ya", "inner", wa_codes, wa_plane, *quantize(f"x{c}", xb[c][:]))
+            products(ya, c, "ya", "inner", wa_codes, wa_plane[WA_ROW:, :], *quantize(f"x{c}", xb[c][:]))
 
         def join(c):
             for s in range(halves):

@@ -29,6 +29,7 @@ RUN = 8
 BLOCKS = J // P
 WB_ROW = 4
 WA_ROW = 8
+STAGE = P - 16
 
 
 def tile_list_htabg_gate_resP_kernel(
@@ -38,6 +39,7 @@ def tile_list_htabg_gate_resP_kernel(
     nc = tc.nc
     with ExitStack() as ctx:
         keep = ctx.enter_context(tc.tile_pool(name="keep", bufs=1))
+        ring = ctx.enter_context(tc.tile_pool(name="ring", bufs=1))
         psum = ctx.enter_context(tc.psum_pool(name="psum", bufs=4))
 
         def sb(name, shape, dtype, tag=None):
@@ -50,53 +52,57 @@ def tile_list_htabg_gate_resP_kernel(
             for r in range(4):
                 nc.sync.dma_start(out=tile[first + r : P : 32, :].bitcast(I32), in_=scales[0, r:16:4, :].bitcast(I32))
 
+        def placed(name, shape, dtype, offset):
+            return ring.tile(shape, dtype, name=name, tag=name, offset=offset * 1024, align_bytes=64)
+
         tab_list = sb("tab_list", [P, J // 16], U16)
         head_lists = sb("head_lists", [P, J // 16], U16)
-        tabw = sb("tabw", [P, T], I32)
-        tabs = sb("tabs", [P, T], U8)
-        was_raw = sb("was_raw", [P, R], U8)
-        wbs_raw = sb("wbs_raw", [P, R], U8)
-        wa_raw = sb("wa_raw", [P, R], I32)
+        ws_raw = sb("ws_raw", [P, R], U8)
         wb_raw = sb("wb_raw", [P, R], I32)
         wgt = sb("wgt", [P, J], F32)
-        x = [sb(f"x{t}", [P, T], F32) for t in range(PACK)]
-        wd_raw = sb("wd_raw", [P, PACK, N], F32)
-        res_sb = [sb(f"res{u}", [P, PACK, J // 2], F32) for u in range(2)]
-
         wgt_rows = sb("wgt_rows", [P, P], F32)
         identity = sb("identity", [P, P], F32)
-        nc.vector.memset(tabs[:].bitcast(I32), 0)
-        nc.vector.memset(wgt_rows[:], 0.0)
+        tabw = placed("tabw", [P, T], I32, 0)
+        tabs = placed("tabs", [P, T], U8, 18)
+        x = [placed(f"x{t}", [P, T], F32, (8, 18, 0, 10)[t]) for t in range(PACK)]
+        wa_raw = placed("wa_raw", [P, R], I32, 8)
+        wd_raw = placed("wd_raw", [P, PACK, N], F32, 18)
+        res_sb = [placed(f"res{u}", [P, PACK, J // 2], F32, (0, 10)[u]) for u in range(2)]
+
+        nc.vector.memset(ws_raw[:].bitcast(I32), 0)
+        nc.vector.memset(tabs[:STAGE, :].bitcast(I32), 0)
+        nc.vector.memset(wgt_rows[: P - HEADS * BLOCKS, :], 0.0)
         nc.vector.memset(identity[:], 0.0)
         make_identity(nc, identity[:], nomemset=True)
-        nc.vector.memset(wbs_raw[:].bitcast(I32), 0)
-        nc.vector.memset(was_raw[:].bitcast(I32), 0)
 
         x_rows = xT.rearrange("(p i) t -> p i t", i=PACK)
         wd_rows = wd.rearrange("(b t i) n -> t b i n", t=PACK, i=RUN)
         res_rows = res.rearrange("(p i) j -> p i j", i=PACK)
         nc.sync.dma_start(tab_list[:], offs)
-        nc.sync.dma_start(out=wb_raw[:], in_=words(wb_words))
-        load_scales(tabs, tab_scales)
+        nc.sync.dma_start(out=tabs[STAGE:, :].bitcast(I32), in_=tab_scales[0].bitcast(I32))
         nc.sync.dma_start(
-            out=wgt_rows[: HEADS * BLOCKS, :],
+            out=wgt_rows[P - HEADS * BLOCKS :, :],
             in_=wgt2.rearrange("(g r) (b c) -> g r b c", r=P // HEADS, c=P)[:, 0, :, :],
         )
         nc.sync.dma_start(out=tabw[:], in_=words(tab_words))
         nc.sync.dma_start(head_lists[:], offs2)
-        load_scales(wbs_raw, wb_scales, WB_ROW)
-        for t in range(PACK):
-            nc.sync.dma_start(out=x[t][:], in_=x_rows[:, t, :])
-        nc.sync.dma_start(out=wa_raw[:], in_=words(wa_words))
-        load_scales(was_raw, wa_scales, WA_ROW)
-        for t in range(PACK):
-            nc.sync.dma_start(out=wd_raw[:, t, :], in_=wd_rows[t])
-        for u in range(2):
-            nc.sync.dma_start(out=res_sb[u][:], in_=res_rows[:, :, u * J // 2 : (u + 1) * J // 2])
+        load_scales(ws_raw, wb_scales, WB_ROW)
+        nc.sync.dma_start(out=x[0][:], in_=x_rows[:, 0, :])
+        nc.sync.dma_start(out=wb_raw[:], in_=words(wb_words))
+
+        v_codes = sb("v_codes", [P, J], U32)
+        v_staged = sb("v_staged", [P, J], U8)
+        v_scales = sb("v_scales", [P, J], U8)
+        nc.vector.tensor_copy(v_staged[:], tabs[:].indirect(tab_list[:]))
+        for r in range(4):
+            nc.sync.dma_start(out=v_scales[r:P:32, :].bitcast(I32), in_=v_staged[STAGE + r : P : 4, :].bitcast(I32))
+        nc.sync.dma_start(out=x[1][:], in_=x_rows[:, 1, :])
+        nc.vector.tensor_copy(v_codes[:], tabw[:].bitcast(U32).indirect(tab_list[:]))
+        nc.sync.dma_start(out=x[2][:], in_=x_rows[:, 2, :])
 
         turned = psum.tile([P, P], F32, name="turned", tag="inner")
         nc.tensor.transpose(turned[:], wgt_rows[:], identity[:])
-        by_head = turned[:, : HEADS * BLOCKS].rearrange("c (g b) -> c b g", b=BLOCKS)
+        by_head = turned[:, P - HEADS * BLOCKS :].rearrange("c (g b) -> c b g", b=BLOCKS)
         spread = sb("spread", [P, BLOCKS, HEADS, P // HEADS], F32)
         for half in range(2):
             blocks = slice(half * PACK, (half + 1) * PACK)
@@ -114,24 +120,19 @@ def tile_list_htabg_gate_resP_kernel(
                 out=wgt[:, half * BANK : (half + 1) * BANK], in_=back[:].rearrange("p i c -> p (i c)")
             )
 
-        v_codes = sb("v_codes", [P, J], U32)
-        v_scales = sb("v_scales", [P, J], U8)
-        nc.vector.tensor_copy(v_scales[:], tabs[:].indirect(tab_list[:]))
-        nc.vector.tensor_copy(v_codes[:], tabw[:].bitcast(U32).indirect(tab_list[:]))
-
         wa_codes = sb("wa_codes", [P, R], I32)
-        wb_codes = sb("wb_codes", [P, R], I32)
+        wb_codes = sb("wb_codes", [P, R], I32, tag="spread")
         wa_plane = sb("wa_plane", [P, R], U8)
         wb_plane = sb("wb_plane", [P, R], U8)
 
-        def deal(dst, src, run):
-            nc.vector.tensor_copy(
+        def deal(copy, dst, src, run):
+            copy(
                 out=dst.rearrange("p (t b i) -> p t b i", t=PACK, i=run),
                 in_=src.rearrange("p (b t i) -> p t b i", t=PACK, i=run),
             )
 
-        deal(wb_codes[:], wb_raw[:], RUN)
-        deal(wb_plane[:].bitcast(I32), wbs_raw[:].bitcast(I32), RUN // 4)
+        deal(nc.scalar.copy, wb_plane[:].bitcast(U32), ws_raw[:].bitcast(U32), RUN // 4)
+        deal(nc.scalar.copy, wb_codes[:].bitcast(U32), wb_raw[:].bitcast(U32), RUN)
 
         def product(bank, w_codes, w_plane, codes, scales):
             for t in range(PACK):
@@ -151,8 +152,15 @@ def tile_list_htabg_gate_resP_kernel(
             gate.append(g)
 
         picked = sb("picked", [P, PACK, J], F32)
-        for t in range(PACK - 1):
-            nc.vector.tensor_tensor(picked[:, t, :], x[t][:].indirect(head_lists[:]), wgt[:], MULT)
+        nc.vector.tensor_tensor(picked[:, 0, :], x[0][:].indirect(head_lists[:]), wgt[:], MULT)
+        nc.sync.dma_start(out=x[3][:], in_=x_rows[:, 3, :])
+        nc.sync.dma_start(out=wa_raw[:], in_=words(wa_words))
+        load_scales(ws_raw, wa_scales, WA_ROW)
+        nc.vector.tensor_tensor(picked[:, 1, :], x[1][:].indirect(head_lists[:]), wgt[:], MULT)
+        for t in range(PACK):
+            nc.sync.dma_start(out=wd_raw[:, t, :], in_=wd_rows[t])
+        nc.vector.tensor_tensor(picked[:, 2, :], x[2][:].indirect(head_lists[:]), wgt[:], MULT)
+        nc.sync.dma_start(out=res_sb[0][:], in_=res_rows[:, :, : J // 2])
         for c in range(CHUNKS):
             cols = slice(c * CHUNK, (c + 1) * CHUNK)
             nc.vector.tensor_tensor(
@@ -161,8 +169,9 @@ def tile_list_htabg_gate_resP_kernel(
                 wgt[:, cols], MULT,
             )
 
-        deal(wa_codes[:], wa_raw[:], RUN)
-        deal(wa_plane[:].bitcast(I32), was_raw[:].bitcast(I32), RUN // 4)
+        nc.sync.dma_start(out=res_sb[1][:], in_=res_rows[:, :, J // 2 :])
+        deal(nc.vector.tensor_copy, wa_codes[:], wa_raw[:], RUN)
+        deal(nc.vector.tensor_copy, wa_plane[:].bitcast(I32), ws_raw[:].bitcast(I32), RUN // 4)
 
         def weave(woven, planes):
             nc.scalar.copy(

@@ -132,6 +132,7 @@ def tile_list_htabg_gate_resP_kernel(
             )
 
         deal(nc.scalar.copy, wb_plane[:].bitcast(U32), ws_raw[:].bitcast(U32), RUN // 4)
+        load_scales(ws_raw, wa_scales, WA_ROW)
         deal(nc.scalar.copy, wb_codes[:].bitcast(U32), wb_raw[:].bitcast(U32), RUN)
 
         def product(bank, w_codes, w_plane, codes, scales):
@@ -151,27 +152,27 @@ def tile_list_htabg_gate_resP_kernel(
             nc.scalar.activation(g[:], yb[:].rearrange("p t j -> p j t"), SIGMOID)
             gate.append(g)
 
-        picked = sb("picked", [P, PACK, J], F32)
+        deal(nc.scalar.copy, wa_plane[:].bitcast(U32), ws_raw[:].bitcast(U32), RUN // 4)
+
+        picks = sb("picks", [P, PACK * J + CHUNK], F32)
+        picked = picks[:, : PACK * J].rearrange("p (t j) -> p t j", t=PACK)
         nc.vector.tensor_tensor(picked[:, 0, :], x[0][:].indirect(head_lists[:]), wgt[:], MULT)
         nc.sync.dma_start(out=x[3][:], in_=x_rows[:, 3, :])
         nc.sync.dma_start(out=wa_raw[:], in_=words(wa_words))
-        load_scales(ws_raw, wa_scales, WA_ROW)
         nc.vector.tensor_tensor(picked[:, 1, :], x[1][:].indirect(head_lists[:]), wgt[:], MULT)
         for t in range(PACK):
             nc.sync.dma_start(out=wd_raw[:, t, :], in_=wd_rows[t])
         nc.vector.tensor_tensor(picked[:, 2, :], x[2][:].indirect(head_lists[:]), wgt[:], MULT)
         nc.sync.dma_start(out=res_sb[0][:], in_=res_rows[:, :, : J // 2])
-        for c in range(CHUNKS):
-            cols = slice(c * CHUNK, (c + 1) * CHUNK)
+
+        def pick_last(lo, hi):
             nc.vector.tensor_tensor(
-                picked[:, PACK - 1, cols],
-                x[PACK - 1][:].indirect(head_lists[:, c * LIST_COLS : (c + 1) * LIST_COLS]),
-                wgt[:, cols], MULT,
+                picked[:, PACK - 1, lo:hi], x[PACK - 1][:].indirect(head_lists[:, lo // 16 : hi // 16]), wgt[:, lo:hi], MULT
             )
 
-        nc.sync.dma_start(out=res_sb[1][:], in_=res_rows[:, :, J // 2 :])
+        for lo, hi in ((0, UNIT), (UNIT, CHUNK), (CHUNK, 2 * CHUNK), (2 * CHUNK, 3 * CHUNK)):
+            pick_last(lo, hi)
         deal(nc.vector.tensor_copy, wa_codes[:], wa_raw[:], RUN)
-        deal(nc.vector.tensor_copy, wa_plane[:].bitcast(I32), ws_raw[:].bitcast(I32), RUN // 4)
 
         def weave(woven, planes):
             nc.scalar.copy(
@@ -179,9 +180,9 @@ def tile_list_htabg_gate_resP_kernel(
                 in_=planes.rearrange("p t (c i) -> p c t i", i=2),
             )
 
-        def quantize(name, woven):
+        def quantize(name, woven, at=None):
             width = woven.shape[1] // PACK
-            codes = sb(name + "_codes", [P, width], I32)
+            codes = sb(name + "_codes", [P, width], I32) if at is None else placed(name + "_codes", [P, width], I32, at)
             scales = sb(name + "_scales", [P, width], U8)
             nc.vector.quantize_mx(out=codes[:].bitcast(FP8X4), scales=scales[:], in_=woven)
             return codes, scales
@@ -192,9 +193,9 @@ def tile_list_htabg_gate_resP_kernel(
         out_scales = sb("out_scales", [P, J], U8)
         wide = CHUNK * PACK
         halves = CHUNK // UNIT
-        xb = [sb(f"xb{c}", [P, wide], BF16) for c in range(CHUNKS)]
+        xb = [picks[:, PACK * J - CHUNK :].bitcast(BF16)] + [sb(f"xb{c}", [P, wide], BF16)[:] for c in range(1, CHUNKS)]
         hb = [sb(f"hb{c}", [P, wide], BF16) for c in range(CHUNKS)]
-        ob = [sb(f"ob{c}", [P, wide], BF16) for c in range(CHUNKS)]
+        ob = sb("ob", [P, J * PACK], BF16)
         result = [sb(f"result{c}", [P, PACK, CHUNK], F32) for c in range(CHUNKS)]
         ya, y, hq = {}, {}, {}
 
@@ -206,7 +207,7 @@ def tile_list_htabg_gate_resP_kernel(
                 banks[c, s] = bank
 
         def first(c):
-            products(ya, c, "ya", "inner", wa_codes, wa_plane[WA_ROW:, :], *quantize(f"x{c}", xb[c][:]))
+            products(ya, c, "ya", "inner", wa_codes, wa_plane[WA_ROW:, :], *quantize(f"x{c}", xb[c], None if c else 8))
 
         def join(c):
             for s in range(halves):
@@ -229,28 +230,29 @@ def tile_list_htabg_gate_resP_kernel(
                 nc.vector.tensor_tensor(
                     result[c][:, :, cols], y[c, s][:], res_sb[half][:, :, col : col + UNIT], ADD
                 )
-                weave(ob[c][:, s * UNIT * PACK : (s + 1) * UNIT * PACK], result[c][:, :, cols])
+                at = (c * CHUNK + s * UNIT) * PACK
+                weave(ob[:, at : at + UNIT * PACK], result[c][:, :, cols])
             nc.sync.dma_start(out=out_rows[:, :, c * CHUNK : (c + 1) * CHUNK], in_=result[c][:])
 
-        def planes(at, width):
-            c, col = divmod(at, CHUNK)
-            cols = slice(at, at + width)
+        def planes(lo, hi):
             nc.vector.quantize_mx(
-                out=out_codes[:, cols].bitcast(FP8X4), scales=out_scales[:, cols],
-                in_=ob[c][:, col * PACK : (col + width) * PACK],
+                out=out_codes[:, lo:hi].bitcast(FP8X4), scales=out_scales[:, lo:hi], in_=ob[:, lo * PACK : hi * PACK]
             )
-
-        def store_codes(lo, hi):
             nc.sync.dma_start(out=out_words[:, lo:hi], in_=out_codes[:, lo:hi])
 
-        for c in range(CHUNKS):
-            weave(xb[c][:], picked[:, :, c * CHUNK : (c + 1) * CHUNK])
+        for s in range(halves):
+            weave(xb[0][:, s * UNIT * PACK : (s + 1) * UNIT * PACK], picked[:, :, s * UNIT : (s + 1) * UNIT])
+        for c in range(1, CHUNKS - 1):
+            weave(xb[c], picked[:, :, c * CHUNK : (c + 1) * CHUNK])
+        first(0)
+        pick_last(3 * CHUNK, J)
+        nc.sync.dma_start(out=res_sb[1][:], in_=res_rows[:, :, J // 2 :])
+        weave(xb[3], picked[:, :, 3 * CHUNK :])
         wdb = sb("wdb", [P, N * PACK], BF16)
         nc.scalar.copy(
-            out=wdb[:].rearrange("p (t m i) -> p m t i", t=PACK, i=PACK),
-            in_=wd_raw[:].rearrange("p i (m t) -> p m t i", t=PACK),
+            out=wdb[:].rearrange("p (t m e i) -> p m i e t", t=PACK, e=2, i=PACK),
+            in_=wd_raw[:].rearrange("p i (m e t) -> p m i e t", t=PACK, e=2),
         )
-        first(0)
         first(1)
         join(0)
         first(2)
@@ -271,12 +273,8 @@ def tile_list_htabg_gate_resP_kernel(
         second(3)
         add(2)
         add(3)
-        planes(0, CHUNK)
-        planes(CHUNK, CHUNK)
-        planes(2 * CHUNK, CHUNK)
-        store_codes(0, 3 * CHUNK)
-        planes(3 * CHUNK, UNIT)
-        planes(J - UNIT, UNIT)
-        store_codes(3 * CHUNK, J)
+        planes(0, J // 2)
+        planes(J // 2, J - UNIT)
+        planes(J - UNIT, J)
         for r in range(4):
             nc.scalar.dma_start(out=out_2[0, r:16:4, :].bitcast(I32), in_=out_scales[r:P:32, :].bitcast(I32))

@@ -53,7 +53,7 @@ def tile_list_htabg_gate_resP_kernel(
                 nc.sync.dma_start(out=tile[first + r : P : 32, :].bitcast(I32), in_=scales[0, r:16:4, :].bitcast(I32))
 
         def placed(name, shape, dtype, offset):
-            return ring.tile(shape, dtype, name=name, tag=name, offset=offset * 1024, align_bytes=64)
+            return ring.tile(shape, dtype, name=name, tag=name, offset=int(offset * 512), align_bytes=64)
 
         tab_list = sb("tab_list", [P, J // 16], U16)
         head_lists = sb("head_lists", [P, J // 16], U16)
@@ -63,11 +63,12 @@ def tile_list_htabg_gate_resP_kernel(
         wgt_rows = sb("wgt_rows", [P, P], F32)
         identity = sb("identity", [P, P], F32)
         tabw = placed("tabw", [P, T], I32, 0)
-        tabs = placed("tabs", [P, T], U8, 18)
-        x = [placed(f"x{t}", [P, T], F32, (8, 18, 0, 10)[t]) for t in range(PACK)]
-        wa_raw = placed("wa_raw", [P, R], I32, 8)
-        wd_raw = placed("wd_raw", [P, PACK, N], F32, 18)
-        res_sb = [placed(f"res{u}", [P, PACK, J // 2], F32, (0, 10)[u]) for u in range(2)]
+        tabs = placed("tabs", [P, T], U8, 37)
+        x = [placed(f"x{t}", [P, T], F32, (21, 37, 0, 16)[t]) for t in range(PACK)]
+        wa_raw = placed("wa_raw", [P, R], I32, 32)
+        was_raw = placed("was_raw", [P, R], U8, 36)
+        wd_raw = placed("wd_raw", [P, PACK, N], F32, 0)
+        res_sb = [placed(f"res{u}", [P, PACK, J // 2], F32, (16, 37)[u]) for u in range(2)]
 
         nc.vector.memset(ws_raw[:].bitcast(I32), 0)
         nc.vector.memset(tabs[:STAGE, :].bitcast(I32), 0)
@@ -82,7 +83,7 @@ def tile_list_htabg_gate_resP_kernel(
         nc.sync.dma_start(out=tabs[STAGE:, :].bitcast(I32), in_=tab_scales[0].bitcast(I32))
         nc.sync.dma_start(
             out=wgt_rows[P - HEADS * BLOCKS :, :],
-            in_=wgt2.rearrange("(g r) (b c) -> g r b c", r=P // HEADS, c=P)[:, 0, :, :],
+            in_=wgt2.rearrange("p (e c) -> (p e) c", e=2)[0 : 2 * P : 17, :].rearrange("u (b c) -> u b c", c=P),
         )
         nc.sync.dma_start(out=tabw[:], in_=words(tab_words))
         nc.sync.dma_start(head_lists[:], offs2)
@@ -132,7 +133,6 @@ def tile_list_htabg_gate_resP_kernel(
             )
 
         deal(nc.scalar.copy, wb_plane[:].bitcast(U32), ws_raw[:].bitcast(U32), RUN // 4)
-        load_scales(ws_raw, wa_scales, WA_ROW)
         deal(nc.scalar.copy, wb_codes[:].bitcast(U32), wb_raw[:].bitcast(U32), RUN)
 
         def product(bank, w_codes, w_plane, codes, scales):
@@ -152,18 +152,17 @@ def tile_list_htabg_gate_resP_kernel(
             nc.scalar.activation(g[:], yb[:].rearrange("p t j -> p j t"), SIGMOID)
             gate.append(g)
 
-        deal(nc.scalar.copy, wa_plane[:].bitcast(U32), ws_raw[:].bitcast(U32), RUN // 4)
-
         picks = sb("picks", [P, PACK * J + CHUNK], F32)
         picked = picks[:, : PACK * J].rearrange("p (t j) -> p t j", t=PACK)
         nc.vector.tensor_tensor(picked[:, 0, :], x[0][:].indirect(head_lists[:]), wgt[:], MULT)
         nc.sync.dma_start(out=x[3][:], in_=x_rows[:, 3, :])
         nc.sync.dma_start(out=wa_raw[:], in_=words(wa_words))
+        nc.vector.memset(was_raw[:].bitcast(I32), 0)
+        load_scales(was_raw, wa_scales, WA_ROW)
         nc.vector.tensor_tensor(picked[:, 1, :], x[1][:].indirect(head_lists[:]), wgt[:], MULT)
+        nc.vector.tensor_tensor(picked[:, 2, :], x[2][:].indirect(head_lists[:]), wgt[:], MULT)
         for t in range(PACK):
             nc.sync.dma_start(out=wd_raw[:, t, :], in_=wd_rows[t])
-        nc.vector.tensor_tensor(picked[:, 2, :], x[2][:].indirect(head_lists[:]), wgt[:], MULT)
-        nc.sync.dma_start(out=res_sb[0][:], in_=res_rows[:, :, : J // 2])
 
         def pick_last(lo, hi):
             nc.vector.tensor_tensor(
@@ -173,6 +172,7 @@ def tile_list_htabg_gate_resP_kernel(
         for lo, hi in ((0, UNIT), (UNIT, CHUNK), (CHUNK, 2 * CHUNK), (2 * CHUNK, 3 * CHUNK)):
             pick_last(lo, hi)
         deal(nc.vector.tensor_copy, wa_codes[:], wa_raw[:], RUN)
+        deal(nc.vector.tensor_copy, wa_plane[:].bitcast(I32), was_raw[:].bitcast(I32), RUN // 4)
 
         def weave(woven, planes):
             nc.scalar.copy(
@@ -180,10 +180,10 @@ def tile_list_htabg_gate_resP_kernel(
                 in_=planes.rearrange("p t (c i) -> p c t i", i=2),
             )
 
-        def quantize(name, woven, at=None):
+        def quantize(name, woven, at=None, plane_at=None):
             width = woven.shape[1] // PACK
             codes = sb(name + "_codes", [P, width], I32) if at is None else placed(name + "_codes", [P, width], I32, at)
-            scales = sb(name + "_scales", [P, width], U8)
+            scales = sb(name + "_scales", [P, width], U8) if plane_at is None else placed(name + "_scales", [P, width], U8, plane_at)
             nc.vector.quantize_mx(out=codes[:].bitcast(FP8X4), scales=scales[:], in_=woven)
             return codes, scales
 
@@ -207,7 +207,7 @@ def tile_list_htabg_gate_resP_kernel(
                 banks[c, s] = bank
 
         def first(c):
-            products(ya, c, "ya", "inner", wa_codes, wa_plane[WA_ROW:, :], *quantize(f"x{c}", xb[c], None if c else 8))
+            products(ya, c, "ya", "inner", wa_codes, wa_plane[WA_ROW:, :], *quantize(f"x{c}", xb[c], (34.25, 36.75, None, None)[c], 36.25 if c == 2 else None))
 
         def join(c):
             for s in range(halves):
@@ -246,7 +246,7 @@ def tile_list_htabg_gate_resP_kernel(
             weave(xb[c], picked[:, :, c * CHUNK : (c + 1) * CHUNK])
         first(0)
         pick_last(3 * CHUNK, J)
-        nc.sync.dma_start(out=res_sb[1][:], in_=res_rows[:, :, J // 2 :])
+        nc.sync.dma_start(out=res_sb[0][:], in_=res_rows[:, :, : J // 2])
         weave(xb[3], picked[:, :, 3 * CHUNK :])
         wdb = sb("wdb", [P, N * PACK], BF16)
         nc.scalar.copy(
@@ -254,6 +254,7 @@ def tile_list_htabg_gate_resP_kernel(
             in_=wd_raw[:].rearrange("p i (m e t) -> p m i e t", t=PACK, e=2),
         )
         first(1)
+        nc.sync.dma_start(out=res_sb[1][:], in_=res_rows[:, :, J // 2 :])
         join(0)
         first(2)
         join(1)

from contextlib import ExitStack

import concourse.mybir as mybir
from concourse.masks import make_identity

K, L, R, N, T, J = 512, 512, 512, 512, 2048, 1024
FLOPS = 2 * (K * R + L * R + R * N) * J

F32 = mybir.dt.float32
BF16 = mybir.dt.bfloat16
I32 = mybir.dt.int32
U32 = mybir.dt.uint32
U16 = mybir.dt.uint16
U8 = mybir.dt.uint8
FP8X4 = mybir.dt.float8_e4m3fn_x4
MULT = mybir.AluOpType.mult
ADD = mybir.AluOpType.add
SIGMOID = mybir.ActivationFunctionType.Sigmoid

P = 128
PACK = 4
UNIT = 128
CHUNK = 256
BANK = 512
CHUNKS = J // CHUNK
LIST_COLS = CHUNK // 16
HEADS = 8
RUN = 8
BLOCKS = J // P
WB_ROW = 4
WA_ROW = 8
STAGE = P - 16


def tile_list_htabg_gate_resP_kernel(
    tc, tab_words, tab_scales, xT, wgt2, wa_words, wa_scales, wb_words, wb_scales, wd, res, offs, offs2,
    out_0, out_1, out_2,
):
    nc = tc.nc
    with ExitStack() as ctx:
        keep = ctx.enter_context(tc.tile_pool(name="keep", bufs=1))
        ring = ctx.enter_context(tc.tile_pool(name="ring", bufs=1))
        psum = ctx.enter_context(tc.psum_pool(name="psum", bufs=4))

        def sb(name, shape, dtype, tag=None):
            return keep.tile(shape, dtype, name=name, tag=tag or name, align_bytes=64)

        def words(ap):
            return ap[0].rearrange("p c i -> p (c i)").bitcast(I32)

        def load_scales(tile, scales, first=0):
            for r in range(4):
                nc.sync.dma_start(out=tile[first + r : P : 32, :].bitcast(I32), in_=scales[0, r:16:4, :].bitcast(I32))

        def placed(name, shape, dtype, offset):
            return ring.tile(shape, dtype, name=name, tag=name, offset=int(offset * 512), align_bytes=64)

        tab_list = sb("tab_list", [P, J // 16], U16)
        head_lists = sb("head_lists", [P, J // 16], U16)
        ws_raw = sb("ws_raw", [P, R], U8)
        wb_raw = sb("wb_raw", [P, R], I32)
        wgt = sb("wgt", [P, J], F32)
        wgt_rows = sb("wgt_rows", [P, P], F32)
        identity = sb("identity", [P, P], F32)
        tabw = placed("tabw", [P, T], I32, 0)
        tabs = placed("tabs", [P, T], U8, 37)
        x = [placed(f"x{t}", [P, T], F32, (21, 37, 0, 16)[t]) for t in range(PACK)]
        wa_raw = placed("wa_raw", [P, R], I32, 32)
        was_raw = placed("was_raw", [P, R], U8, 36)
        wd_raw = placed("wd_raw", [P, PACK, N], F32, 0)
        res_sb = [placed(f"res{u}", [P, PACK, J // 2], F32, (16, 37)[u]) for u in range(2)]

        nc.vector.memset(ws_raw[:].bitcast(I32), 0)
        nc.vector.memset(tabs[:STAGE, :].bitcast(I32), 0)
        nc.vector.memset(wgt_rows[: P - HEADS * BLOCKS, :], 0.0)
        nc.vector.memset(identity[:], 0.0)
        make_identity(nc, identity[:], nomemset=True)

        x_rows = xT.rearrange("(p i) t -> p i t", i=PACK)
        wd_rows = wd.rearrange("(b t i) n -> t b i n", t=PACK, i=RUN)
        res_rows = res.rearrange("(p i) j -> p i j", i=PACK)
        nc.sync.dma_start(tab_list[:], offs)
        nc.sync.dma_start(out=tabs[STAGE:, :].bitcast(I32), in_=tab_scales[0].bitcast(I32))
        nc.sync.dma_start(
            out=wgt_rows[P - HEADS * BLOCKS :, :],
            in_=wgt2.rearrange("p (e c) -> (p e) c", e=2)[0 : 2 * P : 17, :].rearrange("u (b c) -> u b c", c=P),
        )
        nc.sync.dma_start(out=tabw[:], in_=words(tab_words))
        nc.sync.dma_start(head_lists[:], offs2)
        load_scales(ws_raw, wb_scales, WB_ROW)
        nc.sync.dma_start(out=x[0][:], in_=x_rows[:, 0, :])
        nc.sync.dma_start(out=wb_raw[:], in_=words(wb_words))

        v_codes = sb("v_codes", [P, J], U32)
        v_staged = sb("v_staged", [P, J], U8)
        v_scales = sb("v_scales", [P, J], U8)
        nc.vector.tensor_copy(v_staged[:], tabs[:].indirect(tab_list[:]))
        for r in range(4):
            nc.sync.dma_start(out=v_scales[r:P:32, :].bitcast(I32), in_=v_staged[STAGE + r : P : 4, :].bitcast(I32))
        nc.sync.dma_start(out=x[1][:], in_=x_rows[:, 1, :])
        nc.vector.tensor_copy(v_codes[:], tabw[:].bitcast(U32).indirect(tab_list[:]))
        nc.sync.dma_start(out=x[2][:], in_=x_rows[:, 2, :])

        turned = psum.tile([P, P], F32, name="turned", tag="inner")
        nc.tensor.transpose(turned[:], wgt_rows[:], identity[:])
        by_head = turned[:, P - HEADS * BLOCKS :].rearrange("c (g b) -> c b g", b=BLOCKS)
        spread = sb("spread", [P, BLOCKS, HEADS, P // HEADS], F32)
        for half in range(2):
            blocks = slice(half * PACK, (half + 1) * PACK)
            nc.scalar.copy(
                out=spread[:, blocks, :, :],
                in_=by_head[:, blocks, :].unsqueeze(3).to_broadcast([P, PACK, HEADS, P // HEADS]),
            )
        for half in range(2):
            back = psum.tile([P, PACK, P], F32, name="back", tag="inner")
            for i in range(PACK):
                nc.tensor.transpose(
                    back[:, i, :], spread[:, half * PACK + i, :, :].rearrange("c g r -> c (g r)"), identity[:]
                )
            nc.scalar.copy(
                out=wgt[:, half * BANK : (half + 1) * BANK], in_=back[:].rearrange("p i c -> p (i c)")
            )

        wa_codes = sb("wa_codes", [P, R], I32)
        wb_codes = sb("wb_codes", [P, R], I32, tag="spread")
        wa_plane = sb("wa_plane", [P, R], U8)
        wb_plane = sb("wb_plane", [P, R], U8)

        def deal(copy, dst, src, run):
            copy(
                out=dst.rearrange("p (t b i) -> p t b i", t=PACK, i=run),
                in_=src.rearrange("p (b t i) -> p t b i", t=PACK, i=run),
            )

        deal(nc.scalar.copy, wb_plane[:].bitcast(U32), ws_raw[:].bitcast(U32), RUN // 4)
        deal(nc.scalar.copy, wb_codes[:].bitcast(U32), wb_raw[:].bitcast(U32), RUN)

        def product(bank, w_codes, w_plane, codes, scales):
            for t in range(PACK):
                cols = slice(t * P, (t + 1) * P)
                nc.tensor.matmul_mx(
                    out=bank(t), lhsT=w_codes[:, cols].bitcast(FP8X4), lhsT_scale=w_plane[:, cols],
                    rhs=codes.bitcast(FP8X4), rhs_scale=scales, start=True, stop=True,
                )

        gate = []
        for u in range(J // UNIT):
            cols = slice(u * UNIT, (u + 1) * UNIT)
            yb = psum.tile([P, PACK, UNIT], F32, name="yb", tag="outer")
            product(lambda t: yb[:, t, :], wb_codes, wb_plane[WB_ROW:, :], v_codes[:, cols], v_scales[:, cols])
            g = sb(f"gate{u}", [P, UNIT, PACK], F32)
            nc.scalar.activation(g[:], yb[:].rearrange("p t j -> p j t"), SIGMOID)
            gate.append(g)

        picks = sb("picks", [P, PACK * J + CHUNK], F32)
        picked = picks[:, : PACK * J].rearrange("p (t j) -> p t j", t=PACK)
        nc.vector.tensor_tensor(picked[:, 0, :], x[0][:].indirect(head_lists[:]), wgt[:], MULT)
        nc.sync.dma_start(out=x[3][:], in_=x_rows[:, 3, :])
        nc.sync.dma_start(out=wa_raw[:], in_=words(wa_words))
        nc.vector.memset(was_raw[:].bitcast(I32), 0)
        load_scales(was_raw, wa_scales, WA_ROW)
        nc.vector.tensor_tensor(picked[:, 1, :], x[1][:].indirect(head_lists[:]), wgt[:], MULT)
        nc.vector.tensor_tensor(picked[:, 2, :], x[2][:].indirect(head_lists[:]), wgt[:], MULT)
        for t in range(PACK):
            nc.sync.dma_start(out=wd_raw[:, t, :], in_=wd_rows[t])

        def pick_last(lo, hi):
            nc.vector.tensor_tensor(
                picked[:, PACK - 1, lo:hi], x[PACK - 1][:].indirect(head_lists[:, lo // 16 : hi // 16]), wgt[:, lo:hi], MULT
            )

        for lo, hi in ((0, UNIT), (UNIT, CHUNK), (CHUNK, 2 * CHUNK), (2 * CHUNK, 3 * CHUNK)):
            pick_last(lo, hi)
        deal(nc.vector.tensor_copy, wa_codes[:], wa_raw[:], RUN)
        deal(nc.vector.tensor_copy, wa_plane[:].bitcast(I32), was_raw[:].bitcast(I32), RUN // 4)

        def weave(woven, planes):
            nc.scalar.copy(
                out=woven.rearrange("p (c i t) -> p c t i", t=PACK, i=2),
                in_=planes.rearrange("p t (c i) -> p c t i", i=2),
            )

        def quantize(name, woven, at=None, plane_at=None):
            width = woven.shape[1] // PACK
            codes = sb(name + "_codes", [P, width], I32) if at is None else placed(name + "_codes", [P, width], I32, at)
            scales = sb(name + "_scales", [P, width], U8) if plane_at is None else placed(name + "_scales", [P, width], U8, plane_at)
            nc.vector.quantize_mx(out=codes[:].bitcast(FP8X4), scales=scales[:], in_=woven)
            return codes, scales

        out_rows = out_0.rearrange("(p i) j -> p i j", i=PACK)
        out_words = words(out_1)
        out_codes = sb("out_codes", [P, J], I32)
        out_scales = sb("out_scales", [P, J], U8)
        wide = CHUNK * PACK
        halves = CHUNK // UNIT
        xb = [picks[:, PACK * J - CHUNK :].bitcast(BF16)] + [sb(f"xb{c}", [P, wide], BF16)[:] for c in range(1, CHUNKS)]
        hb = [sb(f"hb{c}", [P, wide], BF16) for c in range(CHUNKS)]
        ob = sb("ob", [P, J * PACK], BF16)
        result = [sb(f"result{c}", [P, PACK, CHUNK], F32) for c in range(CHUNKS)]
        ya, y, hq = {}, {}, {}

        def products(banks, c, name, tag, w_codes, w_plane, codes, scales):
            for s in range(halves):
                cols = slice(s * UNIT, (s + 1) * UNIT)
                bank = psum.tile([P, PACK, UNIT], F32, name=name, tag=tag)
                product(lambda t: bank[:, t, :], w_codes, w_plane, codes[:, cols], scales[:, cols])
                banks[c, s] = bank

        def first(c):
            products(ya, c, "ya", "inner", wa_codes, wa_plane[WA_ROW:, :], *quantize(f"x{c}", xb[c], (34.25, 36.75, None, None)[c], 36.25 if c == 2 else None))

        def join(c):
            for s in range(halves):
                nc.vector.tensor_tensor(
                    hb[c][:, s * UNIT * PACK : (s + 1) * UNIT * PACK].rearrange("p (j t) -> p j t", t=PACK),
                    ya[c, s][:].rearrange("p t j -> p j t"),
                    gate[c * halves + s][:], MULT,
                )

        def quantize_h(c):
            hq[c] = quantize(f"h{c}", hb[c][:])

        def second(c):
            products(y, c, "y", "outer", wd_codes, wd_scales, *hq[c])

        def add(c):
            for s in range(halves):
                cols = slice(s * UNIT, (s + 1) * UNIT)
                half, col = divmod(c * CHUNK + s * UNIT, J // 2)
                nc.vector.tensor_tensor(
                    result[c][:, :, cols], y[c, s][:], res_sb[half][:, :, col : col + UNIT], ADD
                )
                at = (c * CHUNK + s * UNIT) * PACK
                weave(ob[:, at : at + UNIT * PACK], result[c][:, :, cols])
            nc.sync.dma_start(out=out_rows[:, :, c * CHUNK : (c + 1) * CHUNK], in_=result[c][:])

        def planes(lo, hi):
            nc.vector.quantize_mx(
                out=out_codes[:, lo:hi].bitcast(FP8X4), scales=out_scales[:, lo:hi], in_=ob[:, lo * PACK : hi * PACK]
            )
            nc.sync.dma_start(out=out_words[:, lo:hi], in_=out_codes[:, lo:hi])

        for s in range(halves):
            weave(xb[0][:, s * UNIT * PACK : (s + 1) * UNIT * PACK], picked[:, :, s * UNIT : (s + 1) * UNIT])
        for c in range(1, CHUNKS - 1):
            weave(xb[c], picked[:, :, c * CHUNK : (c + 1) * CHUNK])
        first(0)
        pick_last(3 * CHUNK, J)
        nc.sync.dma_start(out=res_sb[0][:], in_=res_rows[:, :, : J // 2])
        weave(xb[3], picked[:, :, 3 * CHUNK :])
        wdb = sb("wdb", [P, N * PACK], BF16)
        nc.scalar.copy(
            out=wdb[:].rearrange("p (t m e i) -> p m i e t", t=PACK, e=2, i=PACK),
            in_=wd_raw[:].rearrange("p i (m e t) -> p m i e t", t=PACK, e=2),
        )
        first(1)
        nc.sync.dma_start(out=res_sb[1][:], in_=res_rows[:, :, J // 2 :])
        join(0)
        first(2)
        join(1)
        first(3)
        quantize_h(0)
        join(2)
        wd_codes, wd_scales = quantize("wd", wdb[:])
        quantize_h(1)
        second(0)
        second(1)
        join(3)
        add(0)
        quantize_h(2)
        second(2)
        add(1)
        quantize_h(3)
        second(3)
        add(2)
        add(3)
        planes(0, J // 2)
        planes(J // 2, J - UNIT)
        planes(J - UNIT, J)
        for r in range(4):
            nc.scalar.dma_start(out=out_2[0, r:16:4, :].bitcast(I32), in_=out_scales[r:P:32, :].bitcast(I32))
